import numpy as np
import ml_dtypes


def mxq(x, axis, fmt="e4m3"):
    dtype, down = {"e4m3": (ml_dtypes.float8_e4m3fn, 7), "e5m2": (ml_dtypes.float8_e5m2, 14)}[fmt]
    v = np.moveaxis(np.asarray(x, np.float32).astype(ml_dtypes.bfloat16).astype(np.float64), axis, -1)
    blocks = v.reshape(v.shape[:-1] + (-1, 32))
    amax = np.abs(blocks).max(-1, keepdims=True)
    byte = np.maximum(np.where(amax > 0, np.frexp(amax)[1] - 1 + 127, 0) - down, 1)
    scale = np.exp2(byte - 127.0)
    codes = (blocks / scale).astype(np.float32).astype(dtype).astype(np.float64)
    return np.moveaxis((codes * scale).reshape(v.shape), -1, axis)


WIDE = False


def mx_kscale(k):
    if not WIDE:
        return np.ones(k)
    levels = np.array([10, -10, 5, -5, 0])
    if k % 512:
        return np.exp2(np.random.permutation(np.resize(levels, k // 32))).repeat(32)
    a = np.empty((k // 512, 16))
    for p in range(k // 512):
        a[p, :8] = np.random.permutation(np.resize(levels, 8))
        for g in range(8):
            far = levels[np.abs(levels - a[p, g]) >= 10]
            a[p, g + 8] = far[np.random.randint(len(far))]
    return np.exp2(a.ravel()).repeat(32)


def f64(x):
    return np.asarray(x).astype(np.float64)


def striped(idx):
    return np.tile(idx.reshape(-1, 16).T, (8, 1)).astype(np.uint16)


def unstriped(offs):
    return offs[:16].T.reshape(-1).astype(np.int64)


E2M1 = np.array([0.0, 0.5, 1.0, 1.5, 2.0, 3.0, 4.0, 6.0, -0.0, -0.5, -1.0, -1.5, -2.0, -3.0, -4.0, -6.0])


def pack_weight(w, fmt):
    k, n = w.shape
    w = f64(np.asarray(w, np.float32).astype(ml_dtypes.bfloat16)).reshape(k // 32, 32, n)
    amax = np.abs(w).max(1)
    if fmt == "e4m3":
        byte = np.frexp(amax)[1] - 1 + 127 - 7
    else:
        mant, ex = np.frexp(amax / 6.0)
        byte = np.where(mant > 0.5, ex, ex - 1) + 127
    byte = np.clip(np.where(amax > 0, byte, 1), 1, 254)
    scaled = (w * np.exp2(127.0 - byte)[:, None, :]).reshape(k, n).astype(np.float32)
    by_word = np.ascontiguousarray(scaled.reshape(k // 512, 128, 4, n).transpose(0, 1, 3, 2))
    if fmt == "e4m3":
        words = by_word.astype(ml_dtypes.float8_e4m3fn).view(np.uint8)
    else:
        c = by_word.astype(ml_dtypes.float4_e2m1fn).view(np.uint8) & 0xF
        words = (c[..., 0::2] | (c[..., 1::2] << 4)).reshape(k // 512, 128, 2 * n)
    return np.ascontiguousarray(words), np.ascontiguousarray(byte.astype(np.uint8).reshape(k // 512, 16, n))


def unpack_weight(words, scales, fmt):
    g, _, n = scales.shape
    words = np.ascontiguousarray(words).reshape(g, 128, n, -1)
    if fmt == "e4m3":
        vals = words.view(ml_dtypes.float8_e4m3fn).astype(np.float64)
    else:
        nib = np.empty((g, 128, n, 4), np.uint8)
        nib[..., 0::2] = words & 0xF
        nib[..., 1::2] = words >> 4
        vals = E2M1[nib]
    vals = vals * np.repeat(np.exp2(scales.astype(np.float64) - 127.0), 8, axis=1)[..., None]
    return vals.transpose(0, 1, 3, 2).reshape(g * 512, n)


def gelu(v):
    return 0.5 * v * (1.0 + np.tanh(np.sqrt(2.0 / np.pi) * (v + 0.044715 * v**3)))


def striped8(idx):
    return np.concatenate([v.reshape(-1, 16).T for v in idx]).astype(np.uint16)


def unstriped8(offs):
    return np.stack([offs[16 * g:16 * g + 16].T.reshape(-1) for g in range(8)]).astype(np.int64)


def heads(h, wgt, idx8):
    r = np.arange(h.shape[0])
    return wgt[r // 4 % 128] * h[r[:, None], idx8[r % 512 // 64]]


def put_heads(h, wgs, idx8, t2):
    r = np.arange(h.shape[0])
    page = np.zeros((h.shape[0], t2))
    page[r[:, None], idx8[r % 512 // 64]] = wgs[r // 4 % 128] * h
    return page


K, T, S, H, P, N, T2 = 1024, 4096, 1024, 1024, 512, 512, 1024

def setup_inputs():
    n = np.random.standard_normal
    s = mx_kscale(K)[:, None]
    u = mx_kscale(H)[:, None]
    d = {}
    d["tab_words"], d["tab_scales"] = pack_weight(n((K, T)) * s, "e4m3")
    d["offs"] = striped(np.random.permutation(T)[:S])
    d["w1"] = (n((K, H)) / s * u.T / K ** 0.5).astype(np.float32)
    d["b1"] = (0.5 * n(H) * u[:, 0]).astype(np.float32)
    d["offs2"] = striped8(np.stack([np.random.permutation(S)[:P] for _ in range(8)]))
    d["wgt"] = np.repeat(np.random.uniform(0.5, 2.0, (8, P)), 16, axis=0).astype(np.float32)
    d["accent"] = np.random.uniform(0.5, 1.5, (H, P)).astype(np.float32)
    d["wy_words"], d["wy_scales"] = pack_weight(0.25 * n((H, N)) / u / H ** 0.5, "e2m1")
    d["ws"] = (0.3 * n((H, N)) / u / H ** 0.5).astype(np.float32)
    d["wc_words"], d["wc_scales"] = pack_weight(0.24 * n((H, N)) / u / H ** 0.5, "e4m3")
    d["bc"] = np.random.uniform(-0.7, 0.7, N).astype(np.float32)
    d["offs3"] = striped8(np.stack([np.random.permutation(T2)[:P] for _ in range(8)]))
    d["wgo"] = np.repeat(np.random.uniform(0.5, 2.0, (8, P)), 16, axis=0).astype(np.float32)
    return d

def reference(tab_words, tab_scales, offs, w1, b1, offs2, wgt, accent, wy_words, wy_scales, ws, wc_words, wc_scales, bc, offs3, wgo):
    v = unpack_weight(tab_words, tab_scales, "e4m3")[:, unstriped(offs)]
    h = (mxq(f64(w1), 0, "e4m3").T @ v) + f64(b1)[:, None]
    x = heads(h, f64(wgt), unstriped8(offs2))
    z = mxq(x * f64(accent), 0, "e4m3")
    y1 = unpack_weight(wy_words, wy_scales, "e2m1").T @ z
    y2 = mxq(f64(ws), 0, "e4m3").T @ z
    y3 = unpack_weight(wc_words, wc_scales, "e4m3").T @ z
    wave = np.sin(y2) * np.cos(y3 + f64(bc)[:, None])
    y = y1 + wave
    return put_heads(y, f64(wgo), unstriped8(offs3), T2)

@@ -1,0 +1,327 @@
+import math
+from contextlib import ExitStack
+
+import concourse.mybir as mybir
+
+K, T, S, H, M, N, T2 = 1024, 4096, 1024, 1024, 512, 512, 1024
+FLOPS = 2 * K * H * S + 3 * 2 * H * N * M
+
+F32 = mybir.dt.float32
+BF16 = mybir.dt.bfloat16
+I32 = mybir.dt.int32
+U32 = mybir.dt.uint32
+U16 = mybir.dt.uint16
+U8 = mybir.dt.uint8
+E4M3 = mybir.dt.float8_e4m3fn_x4
+E2M1 = mybir.dt.float4_e2m1fn_x4
+ALU = mybir.AluOpType
+ACT = mybir.ActivationFunctionType
+
+P = 128
+PACK = 4
+PASS = P * PACK
+BANK = 512
+HALF = M // 2
+TURN = 2.0 * math.pi
+LATE_BYTES = 74 * 1024
+
+
+def tile_list_ballet_phase_tagger_kernel(
+    tc, tab_words, tab_scales, offs, w1, b1, offs2, wgt, accent, wy_words, wy_scales, ws,
+    wc_words, wc_scales, bc, offs3, wgo, out,
+):
+    nc = tc.nc
+    with ExitStack() as ctx:
+        keep = ctx.enter_context(tc.tile_pool(name="keep", bufs=1))
+        woven = ctx.enter_context(tc.tile_pool(name="woven", bufs=3))
+        hpool = ctx.enter_context(tc.tile_pool(name="hpool", bufs=4))
+        phase = ctx.enter_context(tc.tile_pool(name="phase", bufs=2))
+        psum = ctx.enter_context(tc.psum_pool(name="psum", bufs=8))
+
+        def held(name, shape, dtype, tag=""):
+            return keep.tile(shape, dtype, name=name, align_bytes=64, tag=tag or name)
+
+        tab_sc = held("tab_sc", [P, T], U8)
+        nc.vector.memset(tab_sc[:].bitcast(I32), 0)
+        wyc_sc_raw = held("wyc_sc_raw", [P, 2, N], U8)
+        nc.vector.memset(wyc_sc_raw[:].rearrange("p a n -> p (a n)").bitcast(I32), 0)
+
+        def load_weight(pool, w, row0, col0, name="raw", bufs=2):
+            raw = pool.tile([P, PACK, PASS], F32, name=name, bufs=bufs)
+            nc.sync.dma_start(
+                out=raw[:], in_=w[row0 : row0 + PASS, col0 : col0 + PASS].rearrange("(p j) c -> p j c", j=PACK)
+            )
+            return raw
+
+        list1 = keep.tile([P, S // 16], U16, name="list1")
+        nc.sync.dma_start(list1[:], offs)
+        list2 = keep.tile([P, M // 16], U16, name="list2")
+        list3 = keep.tile([P, M // 16], U16, name="list3")
+
+        def load_table(tile, a):
+            nc.sync.dma_start(out=tile[:].bitcast(I32), in_=tab_words[a].rearrange("p t i -> p (t i)").bitcast(I32))
+
+        tab = [held("tab0", [P, T], U32)]
+        nc.sync.dma_start(list2[:], offs2)
+        nc.sync.dma_start(list3[:], offs3)
+        load_table(tab[0], 0)
+        for q in range(4):
+            nc.sync.dma_start(
+                out=tab_sc[32 * q : 32 * q + 8, :].bitcast(I32),
+                in_=tab_scales[:, 4 * q : 4 * q + 4, :].bitcast(I32),
+            )
+        b1_sb = held("b1_sb", [P, 2, PACK], F32)
+        nc.scalar.dma_start(out=b1_sb[:], in_=b1.rearrange("(b p t) -> p b t", b=2, t=PACK))
+        bc_sb = held("bc_sb", [P, PACK], F32)
+        nc.scalar.dma_start(out=bc_sb[:], in_=bc.rearrange("(p t) -> p t", t=PACK))
+        for q in range(4):
+            for row0, scales in ((0, wy_scales), (4, wc_scales)):
+                nc.gpsimd.dma_start(
+                    out=wyc_sc_raw[32 * q + row0 : 32 * q + row0 + 4, :, :].bitcast(I32),
+                    in_=scales[:, 4 * q : 4 * q + 4, :].rearrange("a r n -> r a n").bitcast(I32),
+                )
+
+        with tc.tile_pool(name="gate", bufs=1) as gate:
+            warm = gate.tile([P, LATE_BYTES // 4], F32, name="warm")
+            nc.vector.memset(warm[:, 0:1], 0.0)
+            nc.scalar.activation(warm[:, 0:1], warm[:, 0:1], ACT.Sin)
+        late = ctx.enter_context(tc.tile_pool(name="late", bufs=1))
+        pages = [held("page%d" % t, [P, T2], F32) for t in range(PACK)]
+        for page in pages:
+            nc.vector.memset(page[:], 0.0)
+
+        def held_late(name, shape, dtype):
+            return late.tile(shape, dtype, name=name, align_bytes=64)
+
+        w1_raw = {(0, 0): load_weight(late, w1, 0, 0, "ring", 1)}
+        tab.append(held_late("tab1", [P, T], U32))
+        load_table(tab[1], 1)
+        w1_last = []
+        for u in range(2):
+            part = held_late("w1_last%d" % u, [P, PACK, PASS // 2], F32)
+            nc.sync.dma_start(
+                out=part[:], in_=w1[PASS:, 256 * u : 256 * (u + 1)].rearrange("(p j) c -> p j c", j=PACK)
+            )
+            w1_last.append(part)
+        wgt_sb = held_late("wgt_sb", [P, M], F32)
+        nc.sync.dma_start(out=wgt_sb[:], in_=wgt)
+        for a in range(2):
+            w1_raw[1, a] = load_weight(late, w1, PASS * a, PASS)
+        acc_sb = [load_weight(late, accent, 0, 0, "acc0", 1)]
+        wc_raw = held_late("wc_raw", [P, 2, N], U32)
+        nc.sync.dma_start(out=wc_raw[:].bitcast(I32), in_=wc_words.rearrange("a p n i -> p a (n i)").bitcast(I32))
+        wy_raw = held_late("wy_raw", [P, 2, 2 * N], U8)
+        nc.sync.dma_start(out=wy_raw[:].bitcast(I32), in_=wy_words.rearrange("a p n -> p a n").bitcast(I32))
+        ws_raw = [load_weight(late, ws, 0, 0, "ws0", 1), load_weight(late, ws, PASS, 0, "ring", 1)]
+        acc_sb.append(load_weight(late, accent, PASS, 0))
+        wgo_sb = held_late("wgo_sb", [P, M], F32)
+        nc.sync.dma_start(out=wgo_sb[:], in_=wgo)
+
+        def weave(raw):
+            grouped = woven.tile([P, PACK, P, PACK], BF16, name="grouped", align_bytes=64)
+            nc.scalar.copy(
+                grouped[:].rearrange("p t c j -> p c j t"), raw[:].rearrange("p j (c t) -> p c j t", t=PACK)
+            )
+            return grouped
+
+        def quantise_weight(name, grouped, cuts=(0, PACK)):
+            codes = held(name + "_codes", [P, PASS], U32)
+            scales = held(name + "_scales", [P, PASS], U8)
+            for lo, hi in zip(cuts, cuts[1:]):
+                nc.vector.quantize_mx(
+                    out=codes[:, P * lo : P * hi].bitcast(E4M3), scales=scales[:, P * lo : P * hi],
+                    in_=grouped[:, lo:hi, :, :].rearrange("p t c j -> p (t c j)"),
+                )
+            return codes, scales
+
+        v_sc = held("v_sc", [P, S], U8)
+        v = {}
+
+        def look_up(a):
+            for s in range(2):
+                v[a, s] = held("v%d%d" % (a, s), [P, BANK], U32)
+                nc.vector.tensor_copy(v[a, s][:], tab[a][:].indirect(list1[:, 32 * s : 32 * (s + 1)]))
+
+        look_up(0)
+        nc.vector.tensor_copy(v_sc[:], tab_sc[:].indirect(list1[:]))
+        w1_q = {(0, 0): quantise_weight("w1_00", weave(w1_raw[0, 0]))}
+        look_up(1)
+        grouped = woven.tile([P, PACK, P, PACK], BF16, name="grouped", align_bytes=64)
+        for u, copy in enumerate((nc.scalar.copy, nc.vector.tensor_copy)):
+            copy(
+                grouped[:, :, 64 * u : 64 * (u + 1), :].rearrange("p t c j -> p c j t"),
+                w1_last[u][:].rearrange("p j (c t) -> p c j t", t=PACK),
+            )
+        w1_q[0, 1] = quantise_weight("w1_01", grouped, (0, 1, 2, 4))
+
+        def h_pass(bank, b, t, s, a):
+            codes, scales = w1_q[b, a]
+            cols = slice(P * t, P * (t + 1))
+            nc.tensor.matmul_mx(
+                out=bank[:], lhsT=codes[:, cols].bitcast(E4M3), lhsT_scale=scales[:, cols],
+                rhs=v[a, s][:].bitcast(E4M3), rhs_scale=v_sc[4 * a :, BANK * s : BANK * (s + 1)],
+                start=(a == 0), stop=(a == 1),
+            )
+
+        def h_out(h, bank, b, t, s):
+            nc.scalar.activation(
+                h[:, BANK * s : BANK * (s + 1)], bank[:], ACT.Identity, bias=b1_sb[:, b, t : t + 1]
+            )
+
+        x = [held("x%d" % b, [P, PACK, M], F32) for b in range(2)]
+
+        def pick(h, b, t, lo, hi):
+            nc.vector.tensor_tensor(
+                x[b][:, t, lo:hi], h[:].indirect(list2[:, lo // 16 : hi // 16]), wgt_sb[:, lo:hi], ALU.mult
+            )
+
+        z_bf = [held("z_bf%d" % b, [P, M, PACK], BF16) for b in range(2)]
+        z_codes = [held("z_codes%d" % b, [P, M], U32) for b in range(2)]
+        z_scales = [held("z_scales%d" % b, [P, M], U8) for b in range(2)]
+
+        def accentuate(b, lo, hi):
+            nc.vector.tensor_tensor(
+                z_bf[b][:, lo:hi, :].rearrange("p (c i) j -> p c j i", i=4),
+                x[b][:, :, lo:hi].rearrange("p j (c i) -> p c j i", i=4),
+                acc_sb[b][:, :, lo:hi].rearrange("p j (c i) -> p c j i", i=4),
+                ALU.mult,
+            )
+
+        def quantise_z(b, lo, hi):
+            nc.vector.quantize_mx(
+                out=z_codes[b][:, lo:hi].bitcast(E4M3), scales=z_scales[b][:, lo:hi],
+                in_=z_bf[b][:, lo:hi, :].rearrange("p m j -> p (m j)"),
+            )
+
+        banks = {(t, s): psum.tile([P, BANK], F32, name="bank") for t in range(PACK) for s in range(2)}
+        for a in range(2):
+            for t in range(PACK):
+                for s in range(2):
+                    h_pass(banks[t, s], 0, t, s, a)
+        h0 = [hpool.tile([P, S], F32, name="h") for t in range(PACK)]
+        h_out(h0[0], banks[0, 0], 0, 0, 0)
+        nc.vector.tensor_scalar(h0[0][:, BANK:], banks[0, 1][:], b1_sb[:, 0, 0:1], None, ALU.add)
+        for t in range(1, PACK):
+            for s in range(2):
+                h_out(h0[t], banks[t, s], 0, t, s)
+        w1_woven = [weave(w1_raw[1, a]) for a in range(2)]
+        for t in range(PACK):
+            pick(h0[t], 0, t, 0, M)
+        w1_q[1, 0] = quantise_weight("w1_10", w1_woven[0])
+        accentuate(0, 0, M)
+        w1_q[1, 1] = quantise_weight("w1_11", w1_woven[1])
+        quantise_z(0, 0, M)
+
+        h1 = []
+        for t in range(PACK):
+            h = hpool.tile([P, S], F32, name="h")
+            for s in range(2):
+                bank = psum.tile([P, BANK], F32, name="bank")
+                for a in range(2):
+                    h_pass(bank, 1, t, s, a)
+                h_out(h, bank, 1, t, s)
+            h1.append(h)
+
+        wc_codes = held("wc_codes", [P, 2, PACK, P], U32)
+        nc.vector.tensor_copy(
+            wc_codes[:].rearrange("p a t c -> p a c t"), wc_raw[:].rearrange("p a (c t) -> p a c t", t=PACK)
+        )
+        wy_codes = held("wy_codes", [P, 2, PACK, 2 * P], U8)
+        nc.vector.tensor_copy(
+            wy_codes[:].bitcast(U16).rearrange("p a t c -> p a c t"),
+            wy_raw[:].bitcast(U16).rearrange("p a (c t) -> p a c t", t=PACK),
+        )
+        wyc_sc = held("wyc_sc", [P, 2, PACK, P], U8, tag="w1_10_codes")
+        nc.vector.tensor_copy(wyc_sc[:], wyc_sc_raw[:].rearrange("p a (c t) -> p a t c", t=PACK))
+        bc_turns = held("bc_turns", [P, PACK], F32)
+        nc.vector.tensor_scalar(bc_turns[:], bc_sb[:], 1.0 / TURN, None, ALU.mult)
+
+        ws_woven = [weave(ws_raw[b]) for b in range(2)]
+        for t in (0, 1):
+            pick(h1[t], 1, t, 0, M)
+        ws_q = [quantise_weight("ws0", ws_woven[0])]
+        for t in (2, 3):
+            pick(h1[t], 1, t, 0, HALF)
+        accentuate(1, 0, HALF)
+        ws_q.append(quantise_weight("ws1", ws_woven[1]))
+        quantise_z(1, 0, HALF)
+        for t in (2, 3):
+            pick(h1[t], 1, t, HALF, M)
+        accentuate(1, HALF, M)
+        quantise_z(1, HALF, M)
+
+        def product(dst, operand, t, lo, hi):
+            for b in range(2):
+                codes, scales = operand(b, t)
+                nc.tensor.matmul_mx(
+                    out=dst, lhsT=codes, lhsT_scale=scales,
+                    rhs=z_codes[b][:, lo:hi].bitcast(E4M3), rhs_scale=z_scales[b][:, lo:hi],
+                    start=(b == 0), stop=(b == 1),
+                )
+
+        def ws_of(b, t):
+            cols = slice(P * t, P * (t + 1))
+            return ws_q[b][0][:, cols].bitcast(E4M3), ws_q[b][1][:, cols]
+
+        def wc_of(b, t):
+            return wc_codes[:, b, t, :].bitcast(E4M3), wyc_sc[4:, b, t, :]
+
+        def wy_of(b, t):
+            return wy_codes[:, b, t, :].bitcast(E2M1), wyc_sc[:, b, t, :]
+
+        def angles(lo, t0):
+            hi = lo + HALF
+            y2 = psum.tile([P, 2, HALF], F32, name="bank")
+            y3 = psum.tile([P, 2, HALF], F32, name="bank")
+            y1 = psum.tile([P, 2, HALF], F32, name="bank")
+            for u in range(2):
+                product(y2[:, u, :], ws_of, t0 + u, lo, hi)
+            for u in range(2):
+                product(y3[:, u, :], wc_of, t0 + u, lo, hi)
+            for u in range(2):
+                for c in range(0, HALF, P):
+                    product(y1[:, u, c : c + P], wy_of, t0 + u, lo + c, lo + c + P)
+            turns = phase.tile([P, 2, 2, HALF], F32, name="turns", bufs=3)
+            nc.scalar.activation(turns[:, 0, :, :], y2[:], ACT.Abs, bias=-0.25, scale=1.0 / TURN)
+            for u in range(2):
+                nc.scalar.activation(
+                    turns[:, 1, u, :], y3[:, u, :], ACT.Abs, bias=bc_turns[:, t0 + u : t0 + u + 1], scale=1.0 / TURN
+                )
+            whole = phase.tile([P, 2, 2, HALF], U32, name="whole")
+            nc.scalar.activation(whole[:], turns[:], ACT.Copy, bias=0.25, scale=1.0)
+            return turns, whole, y1
+
+        def cosines(turns, whole):
+            flat = turns[:].rearrange("p f u m -> p (f u m)")
+            nc.vector.scalar_tensor_tensor(
+                flat, flat, 0.25, whole[:].rearrange("p f u m -> p (f u m)").bitcast(I32), ALU.add, ALU.subtract
+            )
+            nc.scalar.activation(flat, flat, ACT.Sin, scale=TURN)
+
+        def codes_out(turns, y1, lo, t0):
+            wave = phase.tile([P, 2, HALF], F32, name="wave")
+            nc.vector.tensor_tensor(wave[:], turns[:, 0, :, :], turns[:, 1, :, :], ALU.mult)
+            y = phase.tile([P, 2, HALF], F32, name="y")
+            nc.vector.tensor_tensor(y[:], y1[:], wave[:], ALU.add)
+            return y
+
+        def place(y, lo, t0):
+            hi = lo + HALF
+            for u in range(2):
+                t = t0 + u
+                nc.vector.tensor_tensor(
+                    pages[t][:].indirect(list3[:, lo // 16 : hi // 16]), y[:, u, :], wgo_sb[:, lo:hi], ALU.mult
+                )
+                if hi == M:
+                    nc.sync.dma_start(out=out.rearrange("(p t) c -> p t c", t=PACK)[:, t, :], in_=pages[t][:])
+
+        units = [(lo, t0) for lo in (0, HALF) for t0 in (0, 2)]
+        state = [angles(*units[0])]
+        cosines(*state[0][:2])
+        for i, unit in enumerate(units):
+            if i + 1 < len(units):
+                state.append(angles(*units[i + 1]))
+            y = codes_out(state[i][0], state[i][2], *unit)
+            if i + 1 < len(units):
+                cosines(*state[i + 1][:2])
+            place(y, *unit)

@@ -23,7 +23,7 @@ PASS = P * PACK
 BANK = 512
 HALF = M // 2
 TURN = 2.0 * math.pi
-LATE_BYTES = 74 * 1024
+LATE_BYTES = 84 * 1024
 
 
 def tile_list_ballet_phase_tagger_kernel(
@@ -33,7 +33,7 @@ def tile_list_ballet_phase_tagger_kernel(
     nc = tc.nc
     with ExitStack() as ctx:
         keep = ctx.enter_context(tc.tile_pool(name="keep", bufs=1))
-        woven = ctx.enter_context(tc.tile_pool(name="woven", bufs=3))
+        woven = ctx.enter_context(tc.tile_pool(name="woven", bufs=2))
         hpool = ctx.enter_context(tc.tile_pool(name="hpool", bufs=4))
         phase = ctx.enter_context(tc.tile_pool(name="phase", bufs=2))
         psum = ctx.enter_context(tc.psum_pool(name="psum", bufs=8))
@@ -43,8 +43,6 @@ def tile_list_ballet_phase_tagger_kernel(
 
         tab_sc = held("tab_sc", [P, T], U8)
         nc.vector.memset(tab_sc[:].bitcast(I32), 0)
-        wyc_sc_raw = held("wyc_sc_raw", [P, 2, N], U8)
-        nc.vector.memset(wyc_sc_raw[:].rearrange("p a n -> p (a n)").bitcast(I32), 0)
 
         def load_weight(pool, w, row0, col0, name="raw", bufs=2):
             raw = pool.tile([P, PACK, PASS], F32, name=name, bufs=bufs)
@@ -70,22 +68,14 @@ def tile_list_ballet_phase_tagger_kernel(
                 out=tab_sc[32 * q : 32 * q + 8, :].bitcast(I32),
                 in_=tab_scales[:, 4 * q : 4 * q + 4, :].bitcast(I32),
             )
-        b1_sb = held("b1_sb", [P, 2, PACK], F32)
-        nc.scalar.dma_start(out=b1_sb[:], in_=b1.rearrange("(b p t) -> p b t", b=2, t=PACK))
-        bc_sb = held("bc_sb", [P, PACK], F32)
-        nc.scalar.dma_start(out=bc_sb[:], in_=bc.rearrange("(p t) -> p t", t=PACK))
-        for q in range(4):
-            for row0, scales in ((0, wy_scales), (4, wc_scales)):
-                nc.gpsimd.dma_start(
-                    out=wyc_sc_raw[32 * q + row0 : 32 * q + row0 + 4, :, :].bitcast(I32),
-                    in_=scales[:, 4 * q : 4 * q + 4, :].rearrange("a r n -> r a n").bitcast(I32),
-                )
 
         with tc.tile_pool(name="gate", bufs=1) as gate:
             warm = gate.tile([P, LATE_BYTES // 4], F32, name="warm")
             nc.vector.memset(warm[:, 0:1], 0.0)
             nc.scalar.activation(warm[:, 0:1], warm[:, 0:1], ACT.Sin)
         late = ctx.enter_context(tc.tile_pool(name="late", bufs=1))
+        wyc_sc_raw = late.tile([P, 2, N], U8, name="wyc_sc_raw", align_bytes=64)
+        nc.vector.memset(wyc_sc_raw[:].rearrange("p a n -> p (a n)").bitcast(I32), 0)
         pages = [held("page%d" % t, [P, T2], F32) for t in range(PACK)]
         for page in pages:
             nc.vector.memset(page[:], 0.0)
@@ -96,6 +86,8 @@ def tile_list_ballet_phase_tagger_kernel(
         w1_raw = {(0, 0): load_weight(late, w1, 0, 0, "ring", 1)}
         tab.append(held_late("tab1", [P, T], U32))
         load_table(tab[1], 1)
+        b1_sb = held_late("b1_sb", [P, 2, PACK], F32)
+        nc.sync.dma_start(out=b1_sb[:], in_=b1.rearrange("(b p t) -> p b t", b=2, t=PACK))
         w1_last = []
         for u in range(2):
             part = held_late("w1_last%d" % u, [P, PACK, PASS // 2], F32)
@@ -107,19 +99,35 @@ def tile_list_ballet_phase_tagger_kernel(
         nc.sync.dma_start(out=wgt_sb[:], in_=wgt)
         for a in range(2):
             w1_raw[1, a] = load_weight(late, w1, PASS * a, PASS)
+        ws_raw = [load_weight(late, ws, 0, 0, "ws0", 1)]
         acc_sb = [load_weight(late, accent, 0, 0, "acc0", 1)]
+
+        def load_scale_rows(row0, scales):
+            for q in range(4):
+                nc.sync.dma_start(
+                    out=wyc_sc_raw[32 * q + row0 : 32 * q + row0 + 4, :, :].bitcast(I32),
+                    in_=scales[:, 4 * q : 4 * q + 4, :].rearrange("a r n -> r a n").bitcast(I32),
+                )
+
+        load_scale_rows(4, wc_scales)
         wc_raw = held_late("wc_raw", [P, 2, N], U32)
         nc.sync.dma_start(out=wc_raw[:].bitcast(I32), in_=wc_words.rearrange("a p n i -> p a (n i)").bitcast(I32))
         wy_raw = held_late("wy_raw", [P, 2, 2 * N], U8)
         nc.sync.dma_start(out=wy_raw[:].bitcast(I32), in_=wy_words.rearrange("a p n -> p a n").bitcast(I32))
-        ws_raw = [load_weight(late, ws, 0, 0, "ws0", 1), load_weight(late, ws, PASS, 0, "ring", 1)]
-        acc_sb.append(load_weight(late, accent, PASS, 0))
+        load_scale_rows(0, wy_scales)
+        bc_sb = held_late("bc_sb", [P, PACK], F32)
+        nc.sync.dma_start(out=bc_sb[:], in_=bc.rearrange("(p t) -> p t", t=PACK))
+        ws_raw.append(load_weight(late, ws, PASS, 0, "ws1", 1))
         wgo_sb = held_late("wgo_sb", [P, M], F32)
         nc.sync.dma_start(out=wgo_sb[:], in_=wgo)
+        acc_sb.append(load_weight(late, accent, PASS, 0, "ring", 1))
 
-        def weave(raw):
-            grouped = woven.tile([P, PACK, P, PACK], BF16, name="grouped", align_bytes=64)
-            nc.scalar.copy(
+        def weave(raw, copy=nc.scalar.copy, after=""):
+            if after:
+                grouped = held("grouped_" + after, [P, PACK, P, PACK], BF16, tag=after)
+            else:
+                grouped = woven.tile([P, PACK, P, PACK], BF16, name="grouped", align_bytes=64)
+            copy(
                 grouped[:].rearrange("p t c j -> p c j t"), raw[:].rearrange("p j (c t) -> p c j t", t=PACK)
             )
             return grouped
@@ -168,29 +176,28 @@ def tile_list_ballet_phase_tagger_kernel(
                 h[:, BANK * s : BANK * (s + 1)], bank[:], ACT.Identity, bias=b1_sb[:, b, t : t + 1]
             )
 
-        x = [held("x%d" % b, [P, PACK, M], F32) for b in range(2)]
-
-        def pick(h, b, t, lo, hi):
+        def pick(x, h, t, lo, hi):
             nc.vector.tensor_tensor(
-                x[b][:, t, lo:hi], h[:].indirect(list2[:, lo // 16 : hi // 16]), wgt_sb[:, lo:hi], ALU.mult
+                x[:, t, :], h[:].indirect(list2[:, lo // 16 : hi // 16]), wgt_sb[:, lo:hi], ALU.mult
             )
 
-        z_bf = [held("z_bf%d" % b, [P, M, PACK], BF16) for b in range(2)]
         z_codes = [held("z_codes%d" % b, [P, M], U32) for b in range(2)]
         z_scales = [held("z_scales%d" % b, [P, M], U8) for b in range(2)]
 
-        def accentuate(b, lo, hi):
+        def accentuate(name, x, b, lo, hi):
+            z = held(name, [P, hi - lo, PACK], BF16)
             nc.vector.tensor_tensor(
-                z_bf[b][:, lo:hi, :].rearrange("p (c i) j -> p c j i", i=4),
-                x[b][:, :, lo:hi].rearrange("p j (c i) -> p c j i", i=4),
+                z[:].rearrange("p (c i) j -> p c j i", i=4),
+                x[:].rearrange("p j (c i) -> p c j i", i=4),
                 acc_sb[b][:, :, lo:hi].rearrange("p j (c i) -> p c j i", i=4),
                 ALU.mult,
             )
+            return z
 
-        def quantise_z(b, lo, hi):
+        def quantise_z(z, b, lo, hi):
             nc.vector.quantize_mx(
                 out=z_codes[b][:, lo:hi].bitcast(E4M3), scales=z_scales[b][:, lo:hi],
-                in_=z_bf[b][:, lo:hi, :].rearrange("p m j -> p (m j)"),
+                in_=z[:].rearrange("p m j -> p (m j)"),
             )
 
         banks = {(t, s): psum.tile([P, BANK], F32, name="bank") for t in range(PACK) for s in range(2)}
@@ -204,24 +211,32 @@ def tile_list_ballet_phase_tagger_kernel(
         for t in range(1, PACK):
             for s in range(2):
                 h_out(h0[t], banks[t, s], 0, t, s)
-        w1_woven = [weave(w1_raw[1, a]) for a in range(2)]
+        x0 = held("x0", [P, PACK, M], F32)
         for t in range(PACK):
-            pick(h0[t], 0, t, 0, M)
-        w1_q[1, 0] = quantise_weight("w1_10", w1_woven[0])
-        accentuate(0, 0, M)
-        w1_q[1, 1] = quantise_weight("w1_11", w1_woven[1])
-        quantise_z(0, 0, M)
+            pick(x0, h0[t], t, 0, M)
+        w1_woven = [weave(w1_raw[1, 0], after="w1_01_codes"), weave(w1_raw[1, 1], nc.vector.tensor_copy)]
+        for a in range(2):
+            w1_q[1, a] = quantise_weight("w1_1%d" % a, w1_woven[a])
+        ws_woven = [weave(ws_raw[0])]
+        z0 = accentuate("z0", x0, 0, 0, M)
+        ws_q = [quantise_weight("ws0", ws_woven[0])]
+        quantise_z(z0, 0, 0, M)
 
         h1 = []
         for t in range(PACK):
             h = hpool.tile([P, S], F32, name="h")
+            pair = [psum.tile([P, BANK], F32, name="bank") for s in range(2)]
+            for a in range(2):
+                for s in range(2):
+                    h_pass(pair[s], 1, t, s, a)
             for s in range(2):
-                bank = psum.tile([P, BANK], F32, name="bank")
-                for a in range(2):
-                    h_pass(bank, 1, t, s, a)
-                h_out(h, bank, 1, t, s)
+                h_out(h, pair[s], 1, t, s)
             h1.append(h)
 
+        ws_woven.append(weave(ws_raw[1], after="w1_11_codes"))
+        x1_lo = held("x1_lo", [P, PACK, HALF], F32)
+        for t in (0, 1):
+            pick(x1_lo, h1[t], t, 0, HALF)
         wc_codes = held("wc_codes", [P, 2, PACK, P], U32)
         nc.vector.tensor_copy(
             wc_codes[:].rearrange("p a t c -> p a c t"), wc_raw[:].rearrange("p a (c t) -> p a c t", t=PACK)
@@ -231,27 +246,15 @@ def tile_list_ballet_phase_tagger_kernel(
             wy_codes[:].bitcast(U16).rearrange("p a t c -> p a c t"),
             wy_raw[:].bitcast(U16).rearrange("p a (c t) -> p a c t", t=PACK),
         )
+        for t in (2, 3):
+            pick(x1_lo, h1[t], t, 0, HALF)
         wyc_sc = held("wyc_sc", [P, 2, PACK, P], U8, tag="w1_10_codes")
         nc.vector.tensor_copy(wyc_sc[:], wyc_sc_raw[:].rearrange("p a (c t) -> p a t c", t=PACK))
         bc_turns = held("bc_turns", [P, PACK], F32)
         nc.vector.tensor_scalar(bc_turns[:], bc_sb[:], 1.0 / TURN, None, ALU.mult)
 
-        ws_woven = [weave(ws_raw[b]) for b in range(2)]
-        for t in (0, 1):
-            pick(h1[t], 1, t, 0, M)
-        ws_q = [quantise_weight("ws0", ws_woven[0])]
-        for t in (2, 3):
-            pick(h1[t], 1, t, 0, HALF)
-        accentuate(1, 0, HALF)
-        ws_q.append(quantise_weight("ws1", ws_woven[1]))
-        quantise_z(1, 0, HALF)
-        for t in (2, 3):
-            pick(h1[t], 1, t, HALF, M)
-        accentuate(1, HALF, M)
-        quantise_z(1, HALF, M)
-
-        def product(dst, operand, t, lo, hi):
-            for b in range(2):
+        def product(dst, operand, t, lo, hi, blocks=(0, 1)):
+            for b in blocks:
                 codes, scales = operand(b, t)
                 nc.tensor.matmul_mx(
                     out=dst, lhsT=codes, lhsT_scale=scales,
@@ -269,27 +272,29 @@ def tile_list_ballet_phase_tagger_kernel(
         def wy_of(b, t):
             return wy_codes[:, b, t, :].bitcast(E2M1), wyc_sc[:, b, t, :]
 
+        def turns_of(y3, y2, t0):
+            turns = phase.tile([P, 2, 2, HALF], F32, name="turns", bufs=3)
+            for u in range(2):
+                nc.scalar.activation(
+                    turns[:, 1, u, :], y3[u], ACT.Abs, bias=bc_turns[:, t0 + u : t0 + u + 1], scale=1.0 / TURN
+                )
+            for dst, src in y2:
+                nc.scalar.activation(dst(turns), src, ACT.Abs, bias=-0.25, scale=1.0 / TURN)
+            return turns
+
         def angles(lo, t0):
             hi = lo + HALF
-            y2 = psum.tile([P, 2, HALF], F32, name="bank")
             y3 = psum.tile([P, 2, HALF], F32, name="bank")
-            y1 = psum.tile([P, 2, HALF], F32, name="bank")
-            for u in range(2):
-                product(y2[:, u, :], ws_of, t0 + u, lo, hi)
+            y2 = psum.tile([P, 2, HALF], F32, name="bank")
             for u in range(2):
                 product(y3[:, u, :], wc_of, t0 + u, lo, hi)
             for u in range(2):
-                for c in range(0, HALF, P):
-                    product(y1[:, u, c : c + P], wy_of, t0 + u, lo + c, lo + c + P)
-            turns = phase.tile([P, 2, 2, HALF], F32, name="turns", bufs=3)
-            nc.scalar.activation(turns[:, 0, :, :], y2[:], ACT.Abs, bias=-0.25, scale=1.0 / TURN)
-            for u in range(2):
-                nc.scalar.activation(
-                    turns[:, 1, u, :], y3[:, u, :], ACT.Abs, bias=bc_turns[:, t0 + u : t0 + u + 1], scale=1.0 / TURN
-                )
-            whole = phase.tile([P, 2, 2, HALF], U32, name="whole")
+                product(y2[:, u, :], ws_of, t0 + u, lo, hi)
+            return turns_of([y3[:, u, :] for u in range(2)], [(lambda a: a[:, 0, :, :], y2[:])], t0)
+
+        def whole_turns(turns, whole):
             nc.scalar.activation(whole[:], turns[:], ACT.Copy, bias=0.25, scale=1.0)
-            return turns, whole, y1
+            return whole
 
         def cosines(turns, whole):
             flat = turns[:].rearrange("p f u m -> p (f u m)")
@@ -298,12 +303,12 @@ def tile_list_ballet_phase_tagger_kernel(
             )
             nc.scalar.activation(flat, flat, ACT.Sin, scale=TURN)
 
-        def codes_out(turns, y1, lo, t0):
-            wave = phase.tile([P, 2, HALF], F32, name="wave")
-            nc.vector.tensor_tensor(wave[:], turns[:, 0, :, :], turns[:, 1, :, :], ALU.mult)
-            y = phase.tile([P, 2, HALF], F32, name="y")
-            nc.vector.tensor_tensor(y[:], y1[:], wave[:], ALU.add)
-            return y
+        def linear_part(lo, t0):
+            y1 = psum.tile([P, 2, HALF], F32, name="bank")
+            for u in range(2):
+                for c in range(0, HALF, P):
+                    product(y1[:, u, c : c + P], wy_of, t0 + u, lo + c, lo + c + P)
+            return y1
 
         def place(y, lo, t0):
             hi = lo + HALF
@@ -315,13 +320,42 @@ def tile_list_ballet_phase_tagger_kernel(
                 if hi == M:
                     nc.sync.dma_start(out=out.rearrange("(p t) c -> p t c", t=PACK)[:, t, :], in_=pages[t][:])
 
+        early = [(psum.tile([P, HALF], F32, name="bank"), operand, u) for operand in (wc_of, ws_of) for u in range(2)]
+        for bank, operand, u in early:
+            product(bank[:], operand, u, 0, HALF, (0,))
+        z1_lo = accentuate("z1_lo", x1_lo, 1, 0, HALF)
+        ws_q.append(quantise_weight("ws1", ws_woven[1]))
+        quantise_z(z1_lo, 1, 0, HALF)
+        x1_hi = held("x1_hi", [P, PACK, HALF], F32, tag="z1_lo")
+        for t in range(PACK):
+            pick(x1_hi, h1[t], t, HALF, M)
+
         units = [(lo, t0) for lo in (0, HALF) for t0 in (0, 2)]
-        state = [angles(*units[0])]
-        cosines(*state[0][:2])
+        for bank, operand, u in early:
+            product(bank[:], operand, u, 0, HALF, (1,))
+        turns = [turns_of(
+            [early[u][0][:] for u in range(2)],
+            [(lambda a: a[:, 0, 0, :], early[2][0][:]), (lambda a: a[:, 0, 1, :], early[3][0][:])], 0,
+        )]
+
+        def ring():
+            return phase.tile([P, 2, 2, HALF], U32, name="whole")
+
+        whole = [whole_turns(turns[0], held("whole0", [P, 2, 2, HALF], U32, tag="z1_hi"))]
+        turns.append(angles(*units[1]))
+        cosines(turns[0], whole[0])
+        z1_hi = accentuate("z1_hi", x1_hi, 1, HALF, M)
+        quantise_z(z1_hi, 1, HALF, M)
+        whole.append(whole_turns(turns[1], ring()))
         for i, unit in enumerate(units):
+            y1 = linear_part(*unit)
+            wave = phase.tile([P, 2, HALF], F32, name="wave")
+            nc.vector.tensor_tensor(wave[:], turns[i][:, 0, :, :], turns[i][:, 1, :, :], ALU.mult)
             if i + 1 < len(units):
-                state.append(angles(*units[i + 1]))
-            y = codes_out(state[i][0], state[i][2], *unit)
-            if i + 1 < len(units):
-                cosines(*state[i + 1][:2])
+                cosines(turns[i + 1], whole[i + 1])
+            y = phase.tile([P, 2, HALF], F32, name="y")
+            nc.vector.tensor_tensor(y[:], y1[:], wave[:], ALU.add)
+            if i + 2 < len(units):
+                turns.append(angles(*units[i + 2]))
+                whole.append(whole_turns(turns[i + 2], ring()))
             place(y, *unit)

@@ -21,6 +21,8 @@ P = 128
 PACK = 4
 PASS = P * PACK
 BANK = 512
+GROUP = 16
+QUADRANT = 32
 HALF = M // 2
 TURN = 2.0 * math.pi
 LATE_BYTES = 84 * 1024
@@ -34,102 +36,95 @@ def tile_list_ballet_phase_tagger_kernel(
     with ExitStack() as ctx:
         keep = ctx.enter_context(tc.tile_pool(name="keep", bufs=1))
         woven = ctx.enter_context(tc.tile_pool(name="woven", bufs=2))
-        hpool = ctx.enter_context(tc.tile_pool(name="hpool", bufs=4))
+        hpool = ctx.enter_context(tc.tile_pool(name="hpool", bufs=PACK))
         phase = ctx.enter_context(tc.tile_pool(name="phase", bufs=2))
         psum = ctx.enter_context(tc.psum_pool(name="psum", bufs=8))
 
-        def held(name, shape, dtype, tag=""):
-            return keep.tile(shape, dtype, name=name, align_bytes=64, tag=tag or name)
+        def held(name, shape, dtype, after=""):
+            return keep.tile(shape, dtype, name=name, align_bytes=64, tag=after or name)
 
         tab_sc = held("tab_sc", [P, T], U8)
         nc.vector.memset(tab_sc[:].bitcast(I32), 0)
-
-        def load_weight(pool, w, row0, col0, name="raw", bufs=2):
-            raw = pool.tile([P, PACK, PASS], F32, name=name, bufs=bufs)
-            nc.sync.dma_start(
-                out=raw[:], in_=w[row0 : row0 + PASS, col0 : col0 + PASS].rearrange("(p j) c -> p j c", j=PACK)
-            )
-            return raw
-
-        list1 = keep.tile([P, S // 16], U16, name="list1")
-        nc.sync.dma_start(list1[:], offs)
-        list2 = keep.tile([P, M // 16], U16, name="list2")
-        list3 = keep.tile([P, M // 16], U16, name="list3")
+        list1 = keep.tile([P, S // GROUP], U16, name="list1")
+        list2 = keep.tile([P, M // GROUP], U16, name="list2")
+        list3 = keep.tile([P, M // GROUP], U16, name="list3")
+        for tile, source in ((list1, offs), (list2, offs2), (list3, offs3)):
+            nc.sync.dma_start(tile[:], source)
 
         def load_table(tile, a):
             nc.sync.dma_start(out=tile[:].bitcast(I32), in_=tab_words[a].rearrange("p t i -> p (t i)").bitcast(I32))
+            return tile
 
-        tab = [held("tab0", [P, T], U32)]
-        nc.sync.dma_start(list2[:], offs2)
-        nc.sync.dma_start(list3[:], offs3)
-        load_table(tab[0], 0)
+        tab = [load_table(held("tab0", [P, T], U32), 0)]
         for q in range(4):
             nc.sync.dma_start(
-                out=tab_sc[32 * q : 32 * q + 8, :].bitcast(I32),
+                out=tab_sc[QUADRANT * q : QUADRANT * q + 8, :].bitcast(I32),
                 in_=tab_scales[:, 4 * q : 4 * q + 4, :].bitcast(I32),
             )
 
-        with tc.tile_pool(name="gate", bufs=1) as gate:
-            warm = gate.tile([P, LATE_BYTES // 4], F32, name="warm")
-            nc.vector.memset(warm[:, 0:1], 0.0)
-            nc.scalar.activation(warm[:, 0:1], warm[:, 0:1], ACT.Sin)
+        zero = held("zero", [P, 1], F32)
+        with tc.tile_pool(name="opening", bufs=1) as opening:
+            seed = opening.tile([P, LATE_BYTES // 4], F32, name="seed")
+            nc.vector.memset(seed[:, 0:1], 0.0)
+            nc.scalar.activation(zero[:], seed[:, 0:1], ACT.Sin)
         late = ctx.enter_context(tc.tile_pool(name="late", bufs=1))
-        wyc_sc_raw = late.tile([P, 2, N], U8, name="wyc_sc_raw", align_bytes=64)
+
+        def loaded(name, shape, dtype):
+            return late.tile(shape, dtype, name=name, align_bytes=64)
+
+        wyc_sc_raw = loaded("wyc_sc_raw", [P, 2, N], U8)
         nc.vector.memset(wyc_sc_raw[:].rearrange("p a n -> p (a n)").bitcast(I32), 0)
         pages = [held("page%d" % t, [P, T2], F32) for t in range(PACK)]
         for page in pages:
             nc.vector.memset(page[:], 0.0)
 
-        def held_late(name, shape, dtype):
-            return late.tile(shape, dtype, name=name, align_bytes=64)
-
-        w1_raw = {(0, 0): load_weight(late, w1, 0, 0, "ring", 1)}
-        tab.append(held_late("tab1", [P, T], U32))
-        load_table(tab[1], 1)
-        b1_sb = held_late("b1_sb", [P, 2, PACK], F32)
-        nc.sync.dma_start(out=b1_sb[:], in_=b1.rearrange("(b p t) -> p b t", b=2, t=PACK))
-        w1_last = []
-        for u in range(2):
-            part = held_late("w1_last%d" % u, [P, PACK, PASS // 2], F32)
+        def load_rows(name, matrix, row0, col0, width=PASS):
+            tile = late.tile([P, PACK, width], F32, name=name)
             nc.sync.dma_start(
-                out=part[:], in_=w1[PASS:, 256 * u : 256 * (u + 1)].rearrange("(p j) c -> p j c", j=PACK)
+                out=tile[:], in_=matrix[row0 : row0 + PASS, col0 : col0 + width].rearrange("(p j) c -> p j c", j=PACK)
             )
-            w1_last.append(part)
-        wgt_sb = held_late("wgt_sb", [P, M], F32)
-        nc.sync.dma_start(out=wgt_sb[:], in_=wgt)
-        for a in range(2):
-            w1_raw[1, a] = load_weight(late, w1, PASS * a, PASS)
-        ws_raw = [load_weight(late, ws, 0, 0, "ws0", 1)]
-        acc_sb = [load_weight(late, accent, 0, 0, "acc0", 1)]
+            return tile
 
         def load_scale_rows(row0, scales):
             for q in range(4):
                 nc.sync.dma_start(
-                    out=wyc_sc_raw[32 * q + row0 : 32 * q + row0 + 4, :, :].bitcast(I32),
+                    out=wyc_sc_raw[QUADRANT * q + row0 : QUADRANT * q + row0 + 4, :, :].bitcast(I32),
                     in_=scales[:, 4 * q : 4 * q + 4, :].rearrange("a r n -> r a n").bitcast(I32),
                 )
 
+        w1_raw = {(0, 0): load_rows("shared_raw", w1, 0, 0)}
+        tab.append(load_table(loaded("tab1", [P, T], U32), 1))
+        b1_sb = loaded("b1_sb", [P, 2, PACK], F32)
+        nc.sync.dma_start(out=b1_sb[:], in_=b1.rearrange("(b p t) -> p b t", b=2, t=PACK))
+        w1_halves = [load_rows("w1_half%d" % u, w1, PASS, u * PASS // 2, PASS // 2) for u in range(2)]
+        wgt_sb = loaded("wgt_sb", [P, M], F32)
+        nc.sync.dma_start(out=wgt_sb[:], in_=wgt)
+        for a in range(2):
+            w1_raw[1, a] = load_rows("w1_raw1%d" % a, w1, PASS * a, PASS)
+        ws_raw = [load_rows("ws_raw0", ws, 0, 0)]
+        accent_sb = [load_rows("accent0", accent, 0, 0)]
         load_scale_rows(4, wc_scales)
-        wc_raw = held_late("wc_raw", [P, 2, N], U32)
+        wc_raw = loaded("wc_raw", [P, 2, N], U32)
         nc.sync.dma_start(out=wc_raw[:].bitcast(I32), in_=wc_words.rearrange("a p n i -> p a (n i)").bitcast(I32))
-        wy_raw = held_late("wy_raw", [P, 2, 2 * N], U8)
+        wy_raw = loaded("wy_raw", [P, 2, 2 * N], U8)
         nc.sync.dma_start(out=wy_raw[:].bitcast(I32), in_=wy_words.rearrange("a p n -> p a n").bitcast(I32))
         load_scale_rows(0, wy_scales)
-        bc_sb = held_late("bc_sb", [P, PACK], F32)
+        bc_sb = loaded("bc_sb", [P, PACK], F32)
         nc.sync.dma_start(out=bc_sb[:], in_=bc.rearrange("(p t) -> p t", t=PACK))
-        ws_raw.append(load_weight(late, ws, PASS, 0, "ws1", 1))
-        wgo_sb = held_late("wgo_sb", [P, M], F32)
+        ws_raw.append(load_rows("ws_raw1", ws, PASS, 0))
+        wgo_sb = loaded("wgo_sb", [P, M], F32)
         nc.sync.dma_start(out=wgo_sb[:], in_=wgo)
-        acc_sb.append(load_weight(late, accent, PASS, 0, "ring", 1))
+        accent_sb.append(load_rows("shared_raw", accent, PASS, 0))
 
-        def weave(raw, copy=nc.scalar.copy, after=""):
+        def weave(copy, grouped, raw):
+            copy(grouped.rearrange("p t c j -> p c j t"), raw[:].rearrange("p j (c t) -> p c j t", t=PACK))
+
+        def woven_weight(copy, raw, after=""):
             if after:
-                grouped = held("grouped_" + after, [P, PACK, P, PACK], BF16, tag=after)
+                grouped = held("grouped_" + after, [P, PACK, P, PACK], BF16, after)
             else:
                 grouped = woven.tile([P, PACK, P, PACK], BF16, name="grouped", align_bytes=64)
-            copy(
-                grouped[:].rearrange("p t c j -> p c j t"), raw[:].rearrange("p j (c t) -> p c j t", t=PACK)
-            )
+            weave(copy, grouped[:], raw)
             return grouped
 
         def quantise_weight(name, grouped, cuts=(0, PACK)):
@@ -148,19 +143,17 @@ def tile_list_ballet_phase_tagger_kernel(
         def look_up(a):
             for s in range(2):
                 v[a, s] = held("v%d%d" % (a, s), [P, BANK], U32)
-                nc.vector.tensor_copy(v[a, s][:], tab[a][:].indirect(list1[:, 32 * s : 32 * (s + 1)]))
+                entries = list1[:, s * BANK // GROUP : (s + 1) * BANK // GROUP]
+                nc.vector.tensor_copy(v[a, s][:], tab[a][:].indirect(entries))
 
         look_up(0)
         nc.vector.tensor_copy(v_sc[:], tab_sc[:].indirect(list1[:]))
-        w1_q = {(0, 0): quantise_weight("w1_00", weave(w1_raw[0, 0]))}
+        w1_q = {(0, 0): quantise_weight("w1_00", woven_weight(nc.scalar.copy, w1_raw[0, 0]))}
         look_up(1)
-        grouped = woven.tile([P, PACK, P, PACK], BF16, name="grouped", align_bytes=64)
+        last_quarter = woven.tile([P, PACK, P, PACK], BF16, name="grouped", align_bytes=64)
         for u, copy in enumerate((nc.scalar.copy, nc.vector.tensor_copy)):
-            copy(
-                grouped[:, :, 64 * u : 64 * (u + 1), :].rearrange("p t c j -> p c j t"),
-                w1_last[u][:].rearrange("p j (c t) -> p c j t", t=PACK),
-            )
-        w1_q[0, 1] = quantise_weight("w1_01", grouped, (0, 1, 2, 4))
+            weave(copy, last_quarter[:, :, u * P // 2 : (u + 1) * P // 2, :], w1_halves[u])
+        w1_q[0, 1] = quantise_weight("w1_01", last_quarter, (0, 1, 2, PACK))
 
         def h_pass(bank, b, t, s, a):
             codes, scales = w1_q[b, a]
@@ -172,24 +165,22 @@ def tile_list_ballet_phase_tagger_kernel(
             )
 
         def h_out(h, bank, b, t, s):
-            nc.scalar.activation(
-                h[:, BANK * s : BANK * (s + 1)], bank[:], ACT.Identity, bias=b1_sb[:, b, t : t + 1]
-            )
+            nc.scalar.activation(h[:, BANK * s : BANK * (s + 1)], bank[:], ACT.Identity, bias=b1_sb[:, b, t : t + 1])
 
         def pick(x, h, t, lo, hi):
             nc.vector.tensor_tensor(
-                x[:, t, :], h[:].indirect(list2[:, lo // 16 : hi // 16]), wgt_sb[:, lo:hi], ALU.mult
+                x[:, t, :], h[:].indirect(list2[:, lo // GROUP : hi // GROUP]), wgt_sb[:, lo:hi], ALU.mult
             )
 
         z_codes = [held("z_codes%d" % b, [P, M], U32) for b in range(2)]
         z_scales = [held("z_scales%d" % b, [P, M], U8) for b in range(2)]
 
-        def accentuate(name, x, b, lo, hi):
-            z = held(name, [P, hi - lo, PACK], BF16)
+        def accentuate(name, x, b, lo, hi, after=""):
+            z = held(name, [P, hi - lo, PACK], BF16, after)
             nc.vector.tensor_tensor(
                 z[:].rearrange("p (c i) j -> p c j i", i=4),
                 x[:].rearrange("p j (c i) -> p c j i", i=4),
-                acc_sb[b][:, :, lo:hi].rearrange("p j (c i) -> p c j i", i=4),
+                accent_sb[b][:, :, lo:hi].rearrange("p j (c i) -> p c j i", i=4),
                 ALU.mult,
             )
             return z
@@ -214,10 +205,13 @@ def tile_list_ballet_phase_tagger_kernel(
         x0 = held("x0", [P, PACK, M], F32)
         for t in range(PACK):
             pick(x0, h0[t], t, 0, M)
-        w1_woven = [weave(w1_raw[1, 0], after="w1_01_codes"), weave(w1_raw[1, 1], nc.vector.tensor_copy)]
+        w1_woven = [
+            woven_weight(nc.scalar.copy, w1_raw[1, 0], after="w1_01_codes"),
+            woven_weight(nc.vector.tensor_copy, w1_raw[1, 1]),
+        ]
         for a in range(2):
             w1_q[1, a] = quantise_weight("w1_1%d" % a, w1_woven[a])
-        ws_woven = [weave(ws_raw[0])]
+        ws_woven = [woven_weight(nc.scalar.copy, ws_raw[0])]
         z0 = accentuate("z0", x0, 0, 0, M)
         ws_q = [quantise_weight("ws0", ws_woven[0])]
         quantise_z(z0, 0, 0, M)
@@ -233,7 +227,7 @@ def tile_list_ballet_phase_tagger_kernel(
                 h_out(h, pair[s], 1, t, s)
             h1.append(h)
 
-        ws_woven.append(weave(ws_raw[1], after="w1_11_codes"))
+        ws_woven.append(woven_weight(nc.scalar.copy, ws_raw[1], after="w1_11_codes"))
         x1_lo = held("x1_lo", [P, PACK, HALF], F32)
         for t in (0, 1):
             pick(x1_lo, h1[t], t, 0, HALF)
@@ -248,19 +242,10 @@ def tile_list_ballet_phase_tagger_kernel(
         )
         for t in (2, 3):
             pick(x1_lo, h1[t], t, 0, HALF)
-        wyc_sc = held("wyc_sc", [P, 2, PACK, P], U8, tag="w1_10_codes")
+        wyc_sc = held("wyc_sc", [P, 2, PACK, P], U8, after="w1_10_codes")
         nc.vector.tensor_copy(wyc_sc[:], wyc_sc_raw[:].rearrange("p a (c t) -> p a t c", t=PACK))
         bc_turns = held("bc_turns", [P, PACK], F32)
-        nc.vector.tensor_scalar(bc_turns[:], bc_sb[:], 1.0 / TURN, None, ALU.mult)
-
-        def product(dst, operand, t, lo, hi, blocks=(0, 1)):
-            for b in blocks:
-                codes, scales = operand(b, t)
-                nc.tensor.matmul_mx(
-                    out=dst, lhsT=codes, lhsT_scale=scales,
-                    rhs=z_codes[b][:, lo:hi].bitcast(E4M3), rhs_scale=z_scales[b][:, lo:hi],
-                    start=(b == 0), stop=(b == 1),
-                )
+        nc.scalar.activation(bc_turns[:], bc_sb[:], ACT.Copy, scale=1.0 / TURN)
 
         def ws_of(b, t):
             cols = slice(P * t, P * (t + 1))
@@ -272,36 +257,50 @@ def tile_list_ballet_phase_tagger_kernel(
         def wy_of(b, t):
             return wy_codes[:, b, t, :].bitcast(E2M1), wyc_sc[:, b, t, :]
 
-        def turns_of(y3, y2, t0):
-            turns = phase.tile([P, 2, 2, HALF], F32, name="turns", bufs=3)
-            for u in range(2):
-                nc.scalar.activation(
-                    turns[:, 1, u, :], y3[u], ACT.Abs, bias=bc_turns[:, t0 + u : t0 + u + 1], scale=1.0 / TURN
+        def product(dst, weight_of, t, lo, hi, blocks=(0, 1)):
+            for b in blocks:
+                codes, scales = weight_of(b, t)
+                nc.tensor.matmul_mx(
+                    out=dst, lhsT=codes, lhsT_scale=scales,
+                    rhs=z_codes[b][:, lo:hi].bitcast(E4M3), rhs_scale=z_scales[b][:, lo:hi],
+                    start=(b == 0), stop=(b == 1),
                 )
-            for dst, src in y2:
-                nc.scalar.activation(dst(turns), src, ACT.Abs, bias=-0.25, scale=1.0 / TURN)
-            return turns
+
+        def new_turns():
+            return phase.tile([P, 2, 2, HALF], F32, name="turns", bufs=3)
+
+        def y3_turns(dst, y3, t):
+            nc.scalar.activation(dst, y3, ACT.Abs, bias=bc_turns[:, t : t + 1], scale=1.0 / TURN)
+
+        def y2_turns(dst, y2):
+            nc.scalar.activation(dst, y2, ACT.Abs, bias=-0.25, scale=1.0 / TURN)
 
         def angles(lo, t0):
-            hi = lo + HALF
             y3 = psum.tile([P, 2, HALF], F32, name="bank")
             y2 = psum.tile([P, 2, HALF], F32, name="bank")
             for u in range(2):
-                product(y3[:, u, :], wc_of, t0 + u, lo, hi)
+                product(y3[:, u, :], wc_of, t0 + u, lo, lo + HALF)
             for u in range(2):
-                product(y2[:, u, :], ws_of, t0 + u, lo, hi)
-            return turns_of([y3[:, u, :] for u in range(2)], [(lambda a: a[:, 0, :, :], y2[:])], t0)
+                product(y2[:, u, :], ws_of, t0 + u, lo, lo + HALF)
+            turns = new_turns()
+            for u in range(2):
+                y3_turns(turns[:, 1, u, :], y3[:, u, :], t0 + u)
+            y2_turns(turns[:, 0, :, :], y2[:])
+            return turns
 
-        def whole_turns(turns, whole):
+        def round_turns(whole, turns):
             nc.scalar.activation(whole[:], turns[:], ACT.Copy, bias=0.25, scale=1.0)
             return whole
+
+        def new_whole():
+            return phase.tile([P, 2, 2, HALF], U32, name="whole")
 
         def cosines(turns, whole):
             flat = turns[:].rearrange("p f u m -> p (f u m)")
             nc.vector.scalar_tensor_tensor(
                 flat, flat, 0.25, whole[:].rearrange("p f u m -> p (f u m)").bitcast(I32), ALU.add, ALU.subtract
             )
-            nc.scalar.activation(flat, flat, ACT.Sin, scale=TURN)
+            nc.scalar.activation(flat, flat, ACT.Sin, bias=zero[:], scale=TURN)
 
         def linear_part(lo, t0):
             y1 = psum.tile([P, 2, HALF], F32, name="bank")
@@ -315,47 +314,51 @@ def tile_list_ballet_phase_tagger_kernel(
             for u in range(2):
                 t = t0 + u
                 nc.vector.tensor_tensor(
-                    pages[t][:].indirect(list3[:, lo // 16 : hi // 16]), y[:, u, :], wgo_sb[:, lo:hi], ALU.mult
+                    pages[t][:].indirect(list3[:, lo // GROUP : hi // GROUP]), y[:, u, :], wgo_sb[:, lo:hi], ALU.mult
                 )
                 if hi == M:
                     nc.sync.dma_start(out=out.rearrange("(p t) c -> p t c", t=PACK)[:, t, :], in_=pages[t][:])
 
-        early = [(psum.tile([P, HALF], F32, name="bank"), operand, u) for operand in (wc_of, ws_of) for u in range(2)]
-        for bank, operand, u in early:
-            product(bank[:], operand, u, 0, HALF, (0,))
+        first_y3 = [psum.tile([P, HALF], F32, name="bank") for u in range(2)]
+        first_y2 = [psum.tile([P, HALF], F32, name="bank") for u in range(2)]
+
+        def first_unit_passes(b):
+            for tiles, weight_of in ((first_y3, wc_of), (first_y2, ws_of)):
+                for u in range(2):
+                    product(tiles[u][:], weight_of, u, 0, HALF, (b,))
+
+        first_unit_passes(0)
         z1_lo = accentuate("z1_lo", x1_lo, 1, 0, HALF)
-        ws_q.append(quantise_weight("ws1", ws_woven[1]))
         quantise_z(z1_lo, 1, 0, HALF)
-        x1_hi = held("x1_hi", [P, PACK, HALF], F32, tag="z1_lo")
+        ws_q.append(quantise_weight("ws1", ws_woven[1]))
+        x1_hi = held("x1_hi", [P, PACK, HALF], F32, after="z1_lo")
         for t in range(PACK):
             pick(x1_hi, h1[t], t, HALF, M)
 
         units = [(lo, t0) for lo in (0, HALF) for t0 in (0, 2)]
-        for bank, operand, u in early:
-            product(bank[:], operand, u, 0, HALF, (1,))
-        turns = [turns_of(
-            [early[u][0][:] for u in range(2)],
-            [(lambda a: a[:, 0, 0, :], early[2][0][:]), (lambda a: a[:, 0, 1, :], early[3][0][:])], 0,
-        )]
-
-        def ring():
-            return phase.tile([P, 2, 2, HALF], U32, name="whole")
-
-        whole = [whole_turns(turns[0], held("whole0", [P, 2, 2, HALF], U32, tag="z1_hi"))]
+        first_unit_passes(1)
+        turns = [new_turns()]
+        for u in range(2):
+            y3_turns(turns[0][:, 1, u, :], first_y3[u][:], u)
+        for u in range(2):
+            y2_turns(turns[0][:, 0, u, :], first_y2[u][:])
+        whole = [round_turns(held("whole0", [P, 2, 2, HALF], U32), turns[0])]
         turns.append(angles(*units[1]))
         cosines(turns[0], whole[0])
-        z1_hi = accentuate("z1_hi", x1_hi, 1, HALF, M)
+        z1_hi = accentuate("z1_hi", x1_hi, 1, HALF, M, after="whole0")
         quantise_z(z1_hi, 1, HALF, M)
-        whole.append(whole_turns(turns[1], ring()))
+        whole.append(round_turns(new_whole(), turns[1]))
         for i, unit in enumerate(units):
             y1 = linear_part(*unit)
             wave = phase.tile([P, 2, HALF], F32, name="wave")
-            nc.vector.tensor_tensor(wave[:], turns[i][:, 0, :, :], turns[i][:, 1, :, :], ALU.mult)
+            for u in range(2):
+                nc.vector.tensor_tensor(wave[:, u, :], turns[i][:, 0, u, :], turns[i][:, 1, u, :], ALU.mult)
+            y = phase.tile([P, 2, HALF], F32, name="y")
+            for u in range(2):
+                nc.vector.tensor_tensor(y[:, u, :], y1[:, u, :], wave[:, u, :], ALU.add)
             if i + 1 < len(units):
                 cosines(turns[i + 1], whole[i + 1])
-            y = phase.tile([P, 2, HALF], F32, name="y")
-            nc.vector.tensor_tensor(y[:], y1[:], wave[:], ALU.add)
             if i + 2 < len(units):
                 turns.append(angles(*units[i + 2]))
-                whole.append(whole_turns(turns[i + 2], ring()))
+                whole.append(round_turns(new_whole(), turns[i + 2]))
             place(y, *unit)

import math
from contextlib import ExitStack

import concourse.mybir as mybir

K, T, S, H, M, N, T2 = 1024, 4096, 1024, 1024, 512, 512, 1024
FLOPS = 2 * K * H * S + 3 * 2 * H * N * M

F32 = mybir.dt.float32
BF16 = mybir.dt.bfloat16
I32 = mybir.dt.int32
U32 = mybir.dt.uint32
U16 = mybir.dt.uint16
U8 = mybir.dt.uint8
E4M3 = mybir.dt.float8_e4m3fn_x4
E2M1 = mybir.dt.float4_e2m1fn_x4
ALU = mybir.AluOpType
ACT = mybir.ActivationFunctionType

P = 128
PACK = 4
PASS = P * PACK
BANK = 512
GROUP = 16
QUADRANT = 32
HALF = M // 2
TURN = 2.0 * math.pi
LATE_BYTES = 84 * 1024


def tile_list_ballet_phase_tagger_kernel(
    tc, tab_words, tab_scales, offs, w1, b1, offs2, wgt, accent, wy_words, wy_scales, ws,
    wc_words, wc_scales, bc, offs3, wgo, out,
):
    nc = tc.nc
    with ExitStack() as ctx:
        keep = ctx.enter_context(tc.tile_pool(name="keep", bufs=1))
        woven = ctx.enter_context(tc.tile_pool(name="woven", bufs=2))
        hpool = ctx.enter_context(tc.tile_pool(name="hpool", bufs=PACK))
        phase = ctx.enter_context(tc.tile_pool(name="phase", bufs=2))
        psum = ctx.enter_context(tc.psum_pool(name="psum", bufs=8))

        def held(name, shape, dtype, after=""):
            return keep.tile(shape, dtype, name=name, align_bytes=64, tag=after or name)

        tab_sc = held("tab_sc", [P, T], U8)
        nc.vector.memset(tab_sc[:].bitcast(I32), 0)
        list1 = keep.tile([P, S // GROUP], U16, name="list1")
        list2 = keep.tile([P, M // GROUP], U16, name="list2")
        list3 = keep.tile([P, M // GROUP], U16, name="list3")
        for tile, source in ((list1, offs), (list2, offs2), (list3, offs3)):
            nc.sync.dma_start(tile[:], source)

        def load_table(tile, a):
            nc.sync.dma_start(out=tile[:].bitcast(I32), in_=tab_words[a].rearrange("p t i -> p (t i)").bitcast(I32))
            return tile

        tab = [load_table(held("tab0", [P, T], U32), 0)]
        for q in range(4):
            nc.sync.dma_start(
                out=tab_sc[QUADRANT * q : QUADRANT * q + 8, :].bitcast(I32),
                in_=tab_scales[:, 4 * q : 4 * q + 4, :].bitcast(I32),
            )

        zero = held("zero", [P, 1], F32)
        with tc.tile_pool(name="opening", bufs=1) as opening:
            seed = opening.tile([P, LATE_BYTES // 4], F32, name="seed")
            nc.vector.memset(seed[:, 0:1], 0.0)
            nc.scalar.activation(zero[:], seed[:, 0:1], ACT.Sin)
        late = ctx.enter_context(tc.tile_pool(name="late", bufs=1))

        def loaded(name, shape, dtype):
            return late.tile(shape, dtype, name=name, align_bytes=64)

        wyc_sc_raw = loaded("wyc_sc_raw", [P, 2, N], U8)
        nc.vector.memset(wyc_sc_raw[:].rearrange("p a n -> p (a n)").bitcast(I32), 0)
        pages = [held("page%d" % t, [P, T2], F32) for t in range(PACK)]
        for page in pages:
            nc.vector.memset(page[:], 0.0)

        def load_rows(name, matrix, row0, col0, width=PASS):
            tile = late.tile([P, PACK, width], F32, name=name)
            nc.sync.dma_start(
                out=tile[:], in_=matrix[row0 : row0 + PASS, col0 : col0 + width].rearrange("(p j) c -> p j c", j=PACK)
            )
            return tile

        def load_scale_rows(row0, scales):
            for q in range(4):
                nc.sync.dma_start(
                    out=wyc_sc_raw[QUADRANT * q + row0 : QUADRANT * q + row0 + 4, :, :].bitcast(I32),
                    in_=scales[:, 4 * q : 4 * q + 4, :].rearrange("a r n -> r a n").bitcast(I32),
                )

        w1_raw = {(0, 0): load_rows("shared_raw", w1, 0, 0)}
        tab.append(load_table(loaded("tab1", [P, T], U32), 1))
        b1_sb = loaded("b1_sb", [P, 2, PACK], F32)
        nc.sync.dma_start(out=b1_sb[:], in_=b1.rearrange("(b p t) -> p b t", b=2, t=PACK))
        w1_halves = [load_rows("w1_half%d" % u, w1, PASS, u * PASS // 2, PASS // 2) for u in range(2)]
        wgt_sb = loaded("wgt_sb", [P, M], F32)
        nc.sync.dma_start(out=wgt_sb[:], in_=wgt)
        for a in range(2):
            w1_raw[1, a] = load_rows("w1_raw1%d" % a, w1, PASS * a, PASS)
        ws_raw = [load_rows("ws_raw0", ws, 0, 0)]
        accent_sb = [load_rows("accent0", accent, 0, 0)]
        load_scale_rows(4, wc_scales)
        wc_raw = loaded("wc_raw", [P, 2, N], U32)
        nc.sync.dma_start(out=wc_raw[:].bitcast(I32), in_=wc_words.rearrange("a p n i -> p a (n i)").bitcast(I32))
        wy_raw = loaded("wy_raw", [P, 2, 2 * N], U8)
        nc.sync.dma_start(out=wy_raw[:].bitcast(I32), in_=wy_words.rearrange("a p n -> p a n").bitcast(I32))
        load_scale_rows(0, wy_scales)
        bc_sb = loaded("bc_sb", [P, PACK], F32)
        nc.sync.dma_start(out=bc_sb[:], in_=bc.rearrange("(p t) -> p t", t=PACK))
        ws_raw.append(load_rows("ws_raw1", ws, PASS, 0))
        wgo_sb = loaded("wgo_sb", [P, M], F32)
        nc.sync.dma_start(out=wgo_sb[:], in_=wgo)
        accent_sb.append(load_rows("shared_raw", accent, PASS, 0))

        def weave(copy, grouped, raw):
            copy(grouped.rearrange("p t c j -> p c j t"), raw[:].rearrange("p j (c t) -> p c j t", t=PACK))

        def woven_weight(copy, raw, after=""):
            if after:
                grouped = held("grouped_" + after, [P, PACK, P, PACK], BF16, after)
            else:
                grouped = woven.tile([P, PACK, P, PACK], BF16, name="grouped", align_bytes=64)
            weave(copy, grouped[:], raw)
            return grouped

        def quantise_weight(name, grouped, cuts=(0, PACK)):
            codes = held(name + "_codes", [P, PASS], U32)
            scales = held(name + "_scales", [P, PASS], U8)
            for lo, hi in zip(cuts, cuts[1:]):
                nc.vector.quantize_mx(
                    out=codes[:, P * lo : P * hi].bitcast(E4M3), scales=scales[:, P * lo : P * hi],
                    in_=grouped[:, lo:hi, :, :].rearrange("p t c j -> p (t c j)"),
                )
            return codes, scales

        v_sc = held("v_sc", [P, S], U8)
        v = {}

        def look_up(a):
            for s in range(2):
                v[a, s] = held("v%d%d" % (a, s), [P, BANK], U32)
                entries = list1[:, s * BANK // GROUP : (s + 1) * BANK // GROUP]
                nc.vector.tensor_copy(v[a, s][:], tab[a][:].indirect(entries))

        look_up(0)
        nc.vector.tensor_copy(v_sc[:], tab_sc[:].indirect(list1[:]))
        w1_q = {(0, 0): quantise_weight("w1_00", woven_weight(nc.scalar.copy, w1_raw[0, 0]))}
        look_up(1)
        last_quarter = woven.tile([P, PACK, P, PACK], BF16, name="grouped", align_bytes=64)
        for u, copy in enumerate((nc.scalar.copy, nc.vector.tensor_copy)):
            weave(copy, last_quarter[:, :, u * P // 2 : (u + 1) * P // 2, :], w1_halves[u])
        w1_q[0, 1] = quantise_weight("w1_01", last_quarter, (0, 1, 2, PACK))

        def h_pass(bank, b, t, s, a):
            codes, scales = w1_q[b, a]
            cols = slice(P * t, P * (t + 1))
            nc.tensor.matmul_mx(
                out=bank[:], lhsT=codes[:, cols].bitcast(E4M3), lhsT_scale=scales[:, cols],
                rhs=v[a, s][:].bitcast(E4M3), rhs_scale=v_sc[4 * a :, BANK * s : BANK * (s + 1)],
                start=(a == 0), stop=(a == 1),
            )

        def h_out(h, bank, b, t, s):
            nc.scalar.activation(h[:, BANK * s : BANK * (s + 1)], bank[:], ACT.Identity, bias=b1_sb[:, b, t : t + 1])

        def pick(x, h, t, lo, hi):
            nc.vector.tensor_tensor(
                x[:, t, :], h[:].indirect(list2[:, lo // GROUP : hi // GROUP]), wgt_sb[:, lo:hi], ALU.mult
            )

        z_codes = [held("z_codes%d" % b, [P, M], U32) for b in range(2)]
        z_scales = [held("z_scales%d" % b, [P, M], U8) for b in range(2)]

        def accentuate(name, x, b, lo, hi, after=""):
            z = held(name, [P, hi - lo, PACK], BF16, after)
            nc.vector.tensor_tensor(
                z[:].rearrange("p (c i) j -> p c j i", i=4),
                x[:].rearrange("p j (c i) -> p c j i", i=4),
                accent_sb[b][:, :, lo:hi].rearrange("p j (c i) -> p c j i", i=4),
                ALU.mult,
            )
            return z

        def quantise_z(z, b, lo, hi):
            nc.vector.quantize_mx(
                out=z_codes[b][:, lo:hi].bitcast(E4M3), scales=z_scales[b][:, lo:hi],
                in_=z[:].rearrange("p m j -> p (m j)"),
            )

        banks = {(t, s): psum.tile([P, BANK], F32, name="bank") for t in range(PACK) for s in range(2)}
        for a in range(2):
            for t in range(PACK):
                for s in range(2):
                    h_pass(banks[t, s], 0, t, s, a)
        h0 = [hpool.tile([P, S], F32, name="h") for t in range(PACK)]
        h_out(h0[0], banks[0, 0], 0, 0, 0)
        nc.vector.tensor_scalar(h0[0][:, BANK:], banks[0, 1][:], b1_sb[:, 0, 0:1], None, ALU.add)
        for t in range(1, PACK):
            for s in range(2):
                h_out(h0[t], banks[t, s], 0, t, s)
        x0 = held("x0", [P, PACK, M], F32)
        for t in range(PACK):
            pick(x0, h0[t], t, 0, M)
        w1_woven = [
            woven_weight(nc.scalar.copy, w1_raw[1, 0], after="w1_01_codes"),
            woven_weight(nc.vector.tensor_copy, w1_raw[1, 1]),
        ]
        for a in range(2):
            w1_q[1, a] = quantise_weight("w1_1%d" % a, w1_woven[a])
        ws_woven = [woven_weight(nc.scalar.copy, ws_raw[0])]
        z0 = accentuate("z0", x0, 0, 0, M)
        ws_q = [quantise_weight("ws0", ws_woven[0])]
        quantise_z(z0, 0, 0, M)

        h1 = []
        for t in range(PACK):
            h = hpool.tile([P, S], F32, name="h")
            pair = [psum.tile([P, BANK], F32, name="bank") for s in range(2)]
            for a in range(2):
                for s in range(2):
                    h_pass(pair[s], 1, t, s, a)
            for s in range(2):
                h_out(h, pair[s], 1, t, s)
            h1.append(h)

        ws_woven.append(woven_weight(nc.scalar.copy, ws_raw[1], after="w1_11_codes"))
        x1_lo = held("x1_lo", [P, PACK, HALF], F32)
        for t in (0, 1):
            pick(x1_lo, h1[t], t, 0, HALF)
        wc_codes = held("wc_codes", [P, 2, PACK, P], U32)
        nc.vector.tensor_copy(
            wc_codes[:].rearrange("p a t c -> p a c t"), wc_raw[:].rearrange("p a (c t) -> p a c t", t=PACK)
        )
        wy_codes = held("wy_codes", [P, 2, PACK, 2 * P], U8)
        nc.vector.tensor_copy(
            wy_codes[:].bitcast(U16).rearrange("p a t c -> p a c t"),
            wy_raw[:].bitcast(U16).rearrange("p a (c t) -> p a c t", t=PACK),
        )
        for t in (2, 3):
            pick(x1_lo, h1[t], t, 0, HALF)
        wyc_sc = held("wyc_sc", [P, 2, PACK, P], U8, after="w1_10_codes")
        nc.vector.tensor_copy(wyc_sc[:], wyc_sc_raw[:].rearrange("p a (c t) -> p a t c", t=PACK))
        bc_turns = held("bc_turns", [P, PACK], F32)
        nc.scalar.activation(bc_turns[:], bc_sb[:], ACT.Copy, scale=1.0 / TURN)

        def ws_of(b, t):
            cols = slice(P * t, P * (t + 1))
            return ws_q[b][0][:, cols].bitcast(E4M3), ws_q[b][1][:, cols]

        def wc_of(b, t):
            return wc_codes[:, b, t, :].bitcast(E4M3), wyc_sc[4:, b, t, :]

        def wy_of(b, t):
            return wy_codes[:, b, t, :].bitcast(E2M1), wyc_sc[:, b, t, :]

        def product(dst, weight_of, t, lo, hi, blocks=(0, 1)):
            for b in blocks:
                codes, scales = weight_of(b, t)
                nc.tensor.matmul_mx(
                    out=dst, lhsT=codes, lhsT_scale=scales,
                    rhs=z_codes[b][:, lo:hi].bitcast(E4M3), rhs_scale=z_scales[b][:, lo:hi],
                    start=(b == 0), stop=(b == 1),
                )

        def new_turns():
            return phase.tile([P, 2, 2, HALF], F32, name="turns", bufs=3)

        def y3_turns(dst, y3, t):
            nc.scalar.activation(dst, y3, ACT.Abs, bias=bc_turns[:, t : t + 1], scale=1.0 / TURN)

        def y2_turns(dst, y2):
            nc.scalar.activation(dst, y2, ACT.Abs, bias=-0.25, scale=1.0 / TURN)

        def angles(lo, t0):
            y3 = psum.tile([P, 2, HALF], F32, name="bank")
            y2 = psum.tile([P, 2, HALF], F32, name="bank")
            for u in range(2):
                product(y3[:, u, :], wc_of, t0 + u, lo, lo + HALF)
            for u in range(2):
                product(y2[:, u, :], ws_of, t0 + u, lo, lo + HALF)
            turns = new_turns()
            for u in range(2):
                y3_turns(turns[:, 1, u, :], y3[:, u, :], t0 + u)
            y2_turns(turns[:, 0, :, :], y2[:])
            return turns

        def round_turns(whole, turns):
            nc.scalar.activation(whole[:], turns[:], ACT.Copy, bias=0.25, scale=1.0)
            return whole

        def new_whole():
            return phase.tile([P, 2, 2, HALF], U32, name="whole")

        def cosines(turns, whole):
            flat = turns[:].rearrange("p f u m -> p (f u m)")
            nc.vector.scalar_tensor_tensor(
                flat, flat, 0.25, whole[:].rearrange("p f u m -> p (f u m)").bitcast(I32), ALU.add, ALU.subtract
            )
            nc.scalar.activation(flat, flat, ACT.Sin, bias=zero[:], scale=TURN)

        def linear_part(lo, t0):
            y1 = psum.tile([P, 2, HALF], F32, name="bank")
            for u in range(2):
                for c in range(0, HALF, P):
                    product(y1[:, u, c : c + P], wy_of, t0 + u, lo + c, lo + c + P)
            return y1

        def place(y, lo, t0):
            hi = lo + HALF
            for u in range(2):
                t = t0 + u
                nc.vector.tensor_tensor(
                    pages[t][:].indirect(list3[:, lo // GROUP : hi // GROUP]), y[:, u, :], wgo_sb[:, lo:hi], ALU.mult
                )
                if hi == M:
                    nc.sync.dma_start(out=out.rearrange("(p t) c -> p t c", t=PACK)[:, t, :], in_=pages[t][:])

        first_y3 = [psum.tile([P, HALF], F32, name="bank") for u in range(2)]
        first_y2 = [psum.tile([P, HALF], F32, name="bank") for u in range(2)]

        def first_unit_passes(b):
            for tiles, weight_of in ((first_y3, wc_of), (first_y2, ws_of)):
                for u in range(2):
                    product(tiles[u][:], weight_of, u, 0, HALF, (b,))

        first_unit_passes(0)
        z1_lo = accentuate("z1_lo", x1_lo, 1, 0, HALF)
        quantise_z(z1_lo, 1, 0, HALF)
        ws_q.append(quantise_weight("ws1", ws_woven[1]))
        x1_hi = held("x1_hi", [P, PACK, HALF], F32, after="z1_lo")
        for t in range(PACK):
            pick(x1_hi, h1[t], t, HALF, M)

        units = [(lo, t0) for lo in (0, HALF) for t0 in (0, 2)]
        first_unit_passes(1)
        turns = [new_turns()]
        for u in range(2):
            y3_turns(turns[0][:, 1, u, :], first_y3[u][:], u)
        for u in range(2):
            y2_turns(turns[0][:, 0, u, :], first_y2[u][:])
        whole = [round_turns(held("whole0", [P, 2, 2, HALF], U32), turns[0])]
        turns.append(angles(*units[1]))
        cosines(turns[0], whole[0])
        z1_hi = accentuate("z1_hi", x1_hi, 1, HALF, M, after="whole0")
        quantise_z(z1_hi, 1, HALF, M)
        whole.append(round_turns(new_whole(), turns[1]))
        for i, unit in enumerate(units):
            y1 = linear_part(*unit)
            wave = phase.tile([P, 2, HALF], F32, name="wave")
            for u in range(2):
                nc.vector.tensor_tensor(wave[:, u, :], turns[i][:, 0, u, :], turns[i][:, 1, u, :], ALU.mult)
            y = phase.tile([P, 2, HALF], F32, name="y")
            for u in range(2):
                nc.vector.tensor_tensor(y[:, u, :], y1[:, u, :], wave[:, u, :], ALU.add)
            if i + 1 < len(units):
                cosines(turns[i + 1], whole[i + 1])
            if i + 2 < len(units):
                turns.append(angles(*units[i + 2]))
                whole.append(round_turns(new_whole(), turns[i + 2]))
            place(y, *unit)
